import numpy as np
import ml_dtypes


def mxq(x, axis, fmt="e4m3"):
    dtype, down = {"e4m3": (ml_dtypes.float8_e4m3fn, 7), "e5m2": (ml_dtypes.float8_e5m2, 14)}[fmt]
    v = np.moveaxis(np.asarray(x, np.float32).astype(ml_dtypes.bfloat16).astype(np.float64), axis, -1)
    blocks = v.reshape(v.shape[:-1] + (-1, 32))
    amax = np.abs(blocks).max(-1, keepdims=True)
    byte = np.maximum(np.where(amax > 0, np.frexp(amax)[1] - 1 + 127, 0) - down, 1)
    scale = np.exp2(byte - 127.0)
    codes = (blocks / scale).astype(np.float32).astype(dtype).astype(np.float64)
    return np.moveaxis((codes * scale).reshape(v.shape), -1, axis)


WIDE = False


def mx_kscale(k):
    if not WIDE:
        return np.ones(k)
    levels = np.array([10, -10, 5, -5, 0])
    if k % 512:
        return np.exp2(np.random.permutation(np.resize(levels, k // 32))).repeat(32)
    a = np.empty((k // 512, 16))
    for p in range(k // 512):
        a[p, :8] = np.random.permutation(np.resize(levels, 8))
        for g in range(8):
            far = levels[np.abs(levels - a[p, g]) >= 10]
            a[p, g + 8] = far[np.random.randint(len(far))]
    return np.exp2(a.ravel()).repeat(32)


def f64(x):
    return np.asarray(x).astype(np.float64)


def striped(idx):
    return np.tile(idx.reshape(-1, 16).T, (8, 1)).astype(np.uint16)


def unstriped(offs):
    return offs[:16].T.reshape(-1).astype(np.int64)


def striped8(idx):
    return np.concatenate([x.reshape(-1, 16).T for x in idx]).astype(np.uint16)


def runs(offs, k):
    lists = np.stack([offs[16 * r : 16 * r + 16].T.reshape(-1) for r in range(8)]).astype(np.int64)
    return lists[np.arange(k) % 512 // 64]


def pack_weight(w):
    k, n = w.shape
    w = f64(np.asarray(w, np.float32).astype(ml_dtypes.bfloat16)).reshape(k // 32, 32, n)
    amax = np.abs(w).max(1)
    byte = np.clip(np.where(amax > 0, np.frexp(amax)[1] - 1 + 127 - 7, 1), 1, 254)
    scaled = (w * np.exp2(127.0 - byte)[:, None, :]).reshape(k, n).astype(np.float32)
    words = np.ascontiguousarray(scaled.reshape(k // 512, 128, 4, n).transpose(0, 1, 3, 2)).astype(ml_dtypes.float8_e4m3fn).view(np.uint8)
    return words, np.ascontiguousarray(byte.astype(np.uint8).reshape(k // 512, 16, n))


def unpack_weight(words, scales):
    g, p, n, _ = words.shape
    vals = np.ascontiguousarray(words).view(ml_dtypes.float8_e4m3fn).astype(np.float64) * np.repeat(np.exp2(scales.astype(np.float64) - 127.0), 8, axis=1)[..., None]
    return vals.transpose(0, 1, 3, 2).reshape(g * 512, n)


K, T, S, N, G, H, W = 512, 1024, 256, 512, 2048, 512, 1024


def setup_inputs():
    n = np.random.standard_normal
    s = mx_kscale(K)[:, None]
    u = mx_kscale(K)
    packed_xT = pack_weight(n((K, T)) * s)
    packed_dT = pack_weight(n((K, G)) / s)
    return {
        "x_words": packed_xT[0],
        "x_scales": packed_xT[1],
        "d_words": packed_dT[0],
        "d_scales": packed_dT[1],
        "gn": (np.random.uniform(0.5, 1.5, (H, 1)) * u[:, None]).astype(np.float32),
        "gm": (np.random.uniform(0.5, 1.5, (H, 1)) * u[:, None]).astype(np.float32),
        "w1": (n((H, N)) / np.sqrt(2 * H) / u[:, None]).astype(np.float32),
        "w2": (n((H, N)) / np.sqrt(2 * H) / u[:, None]).astype(np.float32),
        "offs": striped(np.random.permutation(T)[:S]),
        "k1": striped8(np.random.randint(0, G, (8, H))),
        "two": striped(np.random.permutation(T)[:S]),
        "n1": striped8(np.stack([np.random.permutation(S) for _ in range(8)])),
        "n2": striped8(np.stack([np.random.permutation(S) for _ in range(8)])),
        "n3": striped(np.random.permutation(S)),
        "n4": striped(np.random.permutation(S)),
        "n5": striped(np.random.randint(0, S, W)),
    }


def reference(x_words, x_scales, d_words, d_scales, gn, gm, w1, w2, offs, k1, two, n1, n2, n3, n4, n5):
    d_k1 = unpack_weight(d_words, d_scales)[np.arange(K)[:, None], runs(k1, K)]
    xq = unpack_weight(x_words, x_scales)[:, unstriped(offs)]
    a = 0.0625 * (d_k1.T @ xq)
    st = a + a[np.arange(H)[:, None], runs(n1, H)]
    z = f64(gn) * (st * (np.tanh(st[np.arange(H)[:, None], runs(n2, H)])))
    x_two = unpack_weight(x_words, x_scales)[:, unstriped(two)]
    b = 0.0625 * (d_k1.T @ x_two)
    st2 = b + 0.5 * b[:, unstriped(n3)]
    z2 = f64(gm) * (st2 - st2[:, unstriped(n4)])
    h = mxq(f64(w1), 0, "e4m3").T @ mxq(z, 0, "e4m3") + mxq(f64(w2), 0, "e4m3").T @ mxq(z2, 0, "e4m3")
    ex = np.exp(h)
    mb = ex[:, unstriped(n5)]
    ms = mb.reshape(N, S, 4).sum(axis=2)
    return np.log(ms + ex) - h

@@ -1,0 +1,236 @@
+from contextlib import ExitStack
+
+import concourse.mybir as mybir
+
+K, T, S, N, G, H, W = 512, 1024, 256, 512, 2048, 512, 1024
+FLOPS = 2 * K * H * S * 2 + 2 * H * N * S * 2
+
+F32 = mybir.dt.float32
+BF16 = mybir.dt.bfloat16
+I32 = mybir.dt.int32
+U32 = mybir.dt.uint32
+U16 = mybir.dt.uint16
+U8 = mybir.dt.uint8
+FP8X4 = mybir.dt.float8_e4m3fn_x4
+ACT = mybir.ActivationFunctionType
+ALU = mybir.AluOpType
+AXIS = mybir.AxisListType
+
+P = 128
+PACK = 4
+HALF = S // 2
+MEMBERS = W // S
+SPARE = 16
+
+
+def tile_picked_kjhopphopglse_none_p_kernel(
+    tc, x_words, x_scales, d_words, d_scales, gn, gm, w1, w2, offs, k1, two, n1, n2, n3, n4, n5, out
+):
+    nc = tc.nc
+    with ExitStack() as ctx:
+        lists = ctx.enter_context(tc.tile_pool(name="lists", bufs=1))
+        keep = ctx.enter_context(tc.tile_pool(name="keep", bufs=1))
+        ring = ctx.enter_context(tc.tile_pool(name="ring", bufs=4))
+        psum = ctx.enter_context(tc.psum_pool(name="psum", bufs=1))
+
+        def load_list(ap, name):
+            tile = lists.tile(list(ap.shape), U16, name=name)
+            nc.sync.dma_start(tile[:], ap)
+            return tile
+
+        d_bytes = keep.tile([P, G], U8, name="d_bytes")
+        x_bytes = keep.tile([P, T], U8, name="x_bytes")
+        d_table = keep.tile([P, G], U32, name="d_table")
+        x_table = keep.tile([P, T], U32, name="x_table", tag="shared_x")
+        k1_t = load_list(k1, "k1_t")
+        nc.sync.dma_start(d_bytes[:].bitcast(I32), d_scales[0].bitcast(I32).unsqueeze(1).to_broadcast([16, 8, G // 4]))
+        two_t = load_list(two, "two_t")
+        nc.sync.dma_start(x_bytes[:].bitcast(I32), x_scales[0].bitcast(I32).unsqueeze(1).to_broadcast([16, 8, T // 4]))
+        offs_t = load_list(offs, "offs_t")
+        n3_t = load_list(n3, "n3_t")
+        n4_t = load_list(n4, "n4_t")
+        nc.sync.dma_start(d_table[:].bitcast(I32), d_words[0].rearrange("p n t -> p (n t)").bitcast(I32))
+        nc.sync.dma_start(x_table[:].bitcast(I32), x_words[0].rearrange("p n t -> p (n t)").bitcast(I32))
+        n1_t = load_list(n1, "n1_t")
+        n2_t = load_list(n2, "n2_t")
+        n5_t = load_list(n5, "n5_t")
+
+        gn_t = keep.tile([P, PACK], F32, name="gn_t")
+        gm_t = keep.tile([P, PACK], F32, name="gm_t")
+        nc.gpsimd.dma_start(gm_t[:], gm.rearrange("(p t) o -> p (t o)", t=PACK))
+        nc.gpsimd.dma_start(gn_t[:], gn.rearrange("(p t) o -> p (t o)", t=PACK))
+
+        placed = keep.tile([P, H + 2 * S], U8, name="placed", align_bytes=64)
+        nc.vector.memset(placed[:].bitcast(I32), 0)
+        b_all = keep.tile([P, (PACK + 1) * S], F32, name="b_all")
+        st2_all = keep.tile([P, (PACK + 1) * S], F32, name="st2_all")
+        a_win = [keep.tile([P, 2 * S], F32, name="a_win%d" % t) for t in range(PACK)]
+        th_win = [keep.tile([P, 2 * S], F32, name="th_win%d" % t, tag="th_win%d" % t, align_bytes=64) for t in range(PACK)]
+        ex_win = [keep.tile([P, W + (S if t == PACK - 1 else SPARE)], F32, name="ex_win%d" % t) for t in range(PACK)]
+        nc.vector.memset(b_all[:, PACK * S :], 0.0)
+        nc.vector.memset(st2_all[:, PACK * S :], 0.0)
+        for t in range(PACK):
+            nc.vector.memset(a_win[t][:, S:], 0.0)
+        for t in range(PACK):
+            nc.vector.memset(ex_win[t][:, S:], 0.0)
+
+        got_bytes = keep.tile([P, H + 2 * S], U8, name="got_bytes", tag="shared", align_bytes=64)
+        nc.vector.tensor_copy(got_bytes[:, 0:H], d_bytes[:].indirect(k1_t[:]))
+        nc.vector.tensor_copy(got_bytes[:, H : H + S], x_bytes[:].indirect(two_t[:]))
+        nc.vector.tensor_copy(got_bytes[:, H + S :], x_bytes[:].indirect(offs_t[:]))
+        for r in range(4):
+            nc.sync.dma_start(placed[r:P:32, :].bitcast(I32), got_bytes[8 * r : P : 32, :].bitcast(I32))
+        got_keys = keep.tile([P, H], U32, name="got_keys")
+        nc.vector.tensor_copy(got_keys[:], d_table[:].indirect(k1_t[:]))
+        key_words = keep.tile([P, H], U32, name="key_words", align_bytes=64)
+        nc.vector.tensor_copy(
+            key_words[:].rearrange("p (t c i) -> p c t i", t=PACK, i=4),
+            got_keys[:].rearrange("p (c i t) -> p c t i", t=PACK, i=4),
+        )
+        two_words = keep.tile([P, S], U32, name="two_words", tag="picked", align_bytes=64)
+        nc.vector.tensor_copy(two_words[:], x_table[:].indirect(two_t[:]))
+        key_bytes = keep.tile([P, H], U8, name="key_bytes", align_bytes=64)
+        nc.vector.tensor_copy(
+            key_bytes[:].rearrange("p (t m) -> p t m", t=PACK),
+            placed[:, 0:H].rearrange("p (m t) -> p t m", t=PACK),
+        )
+
+        w_first = keep.tile([P, 2, PACK, P], F32, name="w_first", tag="shared", align_bytes=64)
+        for side, w in enumerate((w1, w2)):
+            nc.sync.dma_start(w_first[:, side, :, :], w[:, 0:P].rearrange("(p j) m -> p j m", j=PACK))
+
+        def score(words, first_byte, t, tag):
+            acc = psum.tile([P, S], F32, name="acc", tag=tag)
+            rows = slice(P * t, P * (t + 1))
+            nc.tensor.matmul_mx(
+                out=acc[:],
+                lhsT=key_words[:, rows].bitcast(FP8X4),
+                lhsT_scale=key_bytes[:, rows],
+                rhs=words[:].bitcast(FP8X4),
+                rhs_scale=placed[:, first_byte : first_byte + S],
+                start=True,
+                stop=True,
+            )
+            return acc
+
+        def plane(t):
+            return slice(S * t, S * (t + 1))
+
+        def woven(ap):
+            return ap.rearrange("p t (c i) -> p c t i", i=4)
+
+        def planes(tile):
+            return tile[:, 0 : PACK * S].rearrange("p (t j) -> p t j", t=PACK)
+
+        b_acc = [score(two_words, H, t, "low%d" % t) for t in range(PACK)]
+
+        b_n3 = keep.tile([P, PACK * S], F32, name="b_n3")
+        for t in range(PACK):
+            nc.vector.tensor_scalar(b_all[:, plane(t)], b_acc[t][:], gm_t[:, t : t + 1], 0.0625, ALU.mult, ALU.mult)
+        idx_words = keep.tile([P, S], U32, name="idx_words", tag="picked", align_bytes=64)
+        nc.vector.tensor_copy(idx_words[:], x_table[:].indirect(offs_t[:]))
+        a_acc = [score(idx_words, H + S, t, "high%d" % t) for t in range(PACK)]
+        w_rest = keep.tile([P, 2, PACK, N - P], F32, name="w_rest", tag="shared_x")
+        for side, w in enumerate((w1, w2)):
+            nc.sync.dma_start(w_rest[:, side, :, :], w[:, P:].rearrange("(p j) m -> p j m", j=PACK))
+
+        def quantise_weights(mt):
+            raw = w_first[:] if mt == 0 else w_rest[:, :, :, P * (mt - 1) : P * mt]
+            words = ring.tile([P, 2 * P], U32, name="w_words", align_bytes=64)
+            scale_bytes = ring.tile([P, 2 * P], U8, name="w_bytes", align_bytes=64)
+            if mt == 1:
+                grouped = keep.tile([P, 2, P, PACK], BF16, name="grouped1", tag="th_win3", align_bytes=64)
+                for side in range(2):
+                    nc.scalar.copy(
+                        grouped[:, side, :, :].rearrange("p (c i) j -> p c j i", i=4),
+                        raw[:, side, :, :].rearrange("p j (c i) -> p c j i", i=4),
+                    )
+            else:
+                grouped = keep.tile([P, 2, P, PACK], BF16, name="grouped", tag="z_in" if mt else "first", align_bytes=64)
+                nc.vector.tensor_copy(
+                    grouped[:].rearrange("p w (c i) j -> p w c j i", i=4),
+                    raw.rearrange("p w j (c i) -> p w c j i", i=4),
+                )
+            nc.vector.quantize_mx(words[:].bitcast(FP8X4), scale_bytes[:], grouped[:].rearrange("p w m j -> p (w m j)"))
+            return words, scale_bytes
+
+        weights = [quantise_weights(0)]
+        for t in range(PACK):
+            nc.scalar.activation(b_n3[:, plane(t)], b_all[:, S * t : S * (t + 2)].indirect(n3_t[:]), ACT.Copy)
+        st2_n4 = keep.tile([P, PACK * S], F32, name="st2_n4")
+        for u in range(2):
+            pair = slice(2 * S * u, 2 * S * (u + 1))
+            nc.vector.scalar_tensor_tensor(st2_all[:, pair], b_n3[:, pair], 0.5, b_all[:, pair], ALU.mult, ALU.add)
+            for t in ((0,), (1, 2, 3))[u]:
+                nc.vector.tensor_copy(st2_n4[:, plane(t)], st2_all[:, S * t : S * (t + 2)].indirect(n4_t[:]))
+
+        a_n1 = keep.tile([P, PACK * S], F32, name="a_n1")
+        gain_st = keep.tile([P, PACK * S], F32, name="gain_st")
+        th_n2 = keep.tile([P, PACK * S], F32, name="th_n2")
+        for t in range(PACK):
+            nc.scalar.activation(a_win[t][:, 0:S], a_acc[t][:], ACT.Copy, scale=0.0625)
+        for t in range(PACK):
+            nc.scalar.activation(a_n1[:, plane(t)], a_win[t][:].indirect(n1_t[:]), ACT.Copy)
+            nc.vector.tensor_tensor(th_win[t][:, S:], a_win[t][:, 0:S], a_n1[:, plane(t)], ALU.add)
+
+        z2_in = keep.tile([P, S, PACK], BF16, name="z2_in", align_bytes=64)
+        z2_words = keep.tile([P, S], U32, name="z2_words", align_bytes=64)
+        z2_bytes = keep.tile([P, S], U8, name="z2_bytes", align_bytes=64)
+        nc.vector.tensor_tensor(
+            z2_in[:].rearrange("p (c i) t -> p c t i", i=4), woven(planes(st2_all)), woven(planes(st2_n4)), ALU.subtract
+        )
+        for t in range(PACK):
+            nc.scalar.activation(th_win[t][:, 0:S], th_win[t][:, S:], ACT.Tanh)
+            nc.vector.tensor_scalar(gain_st[:, plane(t)], th_win[t][:, S:], gn_t[:, t : t + 1], None, ALU.mult)
+        nc.vector.quantize_mx(z2_words[:].bitcast(FP8X4), z2_bytes[:], z2_in[:].rearrange("p j t -> p (j t)"))
+
+        z_in = keep.tile([P, S, PACK], BF16, name="z_in", tag="z_in", align_bytes=64)
+        z_words = keep.tile([P, S], U32, name="z_words", align_bytes=64)
+        z_bytes = keep.tile([P, S], U8, name="z_bytes", align_bytes=64)
+        for u in range(2):
+            cols = slice(HALF * u, HALF * (u + 1))
+            entries = slice(HALF * u // 16, HALF * (u + 1) // 16)
+            for t in range(PACK):
+                nc.scalar.activation(planes(th_n2)[:, t, cols], th_win[t][:].indirect(n2_t[:, entries]), ACT.Copy)
+            nc.vector.tensor_tensor(
+                z_in[:, cols, :].rearrange("p (c i) t -> p c t i", i=4),
+                woven(planes(gain_st)[:, :, cols]),
+                woven(planes(th_n2)[:, :, cols]),
+                ALU.mult,
+            )
+            nc.vector.quantize_mx(
+                z_words[:, cols].bitcast(FP8X4), z_bytes[:, cols], z_in[:, cols, :].rearrange("p j t -> p (j t)")
+            )
+
+        total = keep.tile([P, PACK * S], F32, name="total")
+        h_acc = []
+        for mt in range(PACK):
+            words, scale_bytes = weights[mt]
+            h = psum.tile([P, S], F32, name="h", tag="low%d" % mt)
+            h_acc.append(h)
+            for side, (rhs, rhs_scale) in ((1, (z2_words, z2_bytes)), (0, (z_words, z_bytes))):
+                cols = slice(P * side, P * (side + 1))
+                nc.tensor.matmul_mx(
+                    out=h[:],
+                    lhsT=words[:, cols].bitcast(FP8X4),
+                    lhsT_scale=scale_bytes[:, cols],
+                    rhs=rhs[:].bitcast(FP8X4),
+                    rhs_scale=rhs_scale[:],
+                    start=(side == 1),
+                    stop=(side == 0),
+                )
+            if mt + 1 < PACK:
+                weights.append(quantise_weights(mt + 1))
+            nc.scalar.activation(ex_win[mt][:, 0:S], h[:], ACT.Exp)
+            sums = ring.tile([P, S], F32, name="sums")
+            members = ring.tile([P, W], F32, name="members")
+            nc.scalar.activation(members[:], ex_win[mt][:].indirect(n5_t[:]), ACT.Copy)
+            nc.vector.tensor_reduce(sums[:], members[:].rearrange("p (j t) -> p j t", t=MEMBERS), AXIS.X, ALU.add)
+            nc.vector.tensor_tensor(total[:, plane(mt)], sums[:], ex_win[mt][:, 0:S], ALU.add)
+
+        logs = ex_win[PACK - 1][:, S:]
+        for mt in range(PACK):
+            nc.scalar.activation(logs[:, plane(mt)], total[:, plane(mt)], ACT.Ln)
+            result = ring.tile([P, S], F32, name="result")
+            nc.vector.tensor_tensor(result[:], logs[:, plane(mt)], h_acc[mt][:], ALU.subtract)
+            nc.sync.dma_start(out[P * mt : P * (mt + 1), :], result[:])

@@ -31,6 +31,7 @@ def tile_picked_kjhopphopglse_none_p_kernel(
         lists = ctx.enter_context(tc.tile_pool(name="lists", bufs=1))
         keep = ctx.enter_context(tc.tile_pool(name="keep", bufs=1))
         ring = ctx.enter_context(tc.tile_pool(name="ring", bufs=4))
+        shared = ctx.enter_context(tc.tile_pool(name="shared", bufs=1))
         psum = ctx.enter_context(tc.psum_pool(name="psum", bufs=1))
 
         def load_list(ap, name):
@@ -59,22 +60,25 @@ def tile_picked_kjhopphopglse_none_p_kernel(
         gm_t = keep.tile([P, PACK], F32, name="gm_t")
         nc.gpsimd.dma_start(gm_t[:], gm.rearrange("(p t) o -> p (t o)", t=PACK))
         nc.gpsimd.dma_start(gn_t[:], gn.rearrange("(p t) o -> p (t o)", t=PACK))
+        gm16 = keep.tile([P, PACK], F32, name="gm16")
+        nc.scalar.activation(gm16[:], gm_t[:], ACT.Copy, scale=0.0625)
 
         placed = keep.tile([P, H + 2 * S], U8, name="placed", align_bytes=64)
         nc.vector.memset(placed[:].bitcast(I32), 0)
-        b_all = keep.tile([P, (PACK + 1) * S], F32, name="b_all")
-        st2_all = keep.tile([P, (PACK + 1) * S], F32, name="st2_all")
-        a_win = [keep.tile([P, 2 * S], F32, name="a_win%d" % t) for t in range(PACK)]
+        b_win = [keep.tile([P, S + SPARE], F32, name="b_win%d" % t) for t in range(PACK)]
+        a_win = [keep.tile([P, 2 * S], F32, name="a_win%d" % t, tag="a_win%d" % t, align_bytes=64) for t in range(PACK)]
         th_win = [keep.tile([P, 2 * S], F32, name="th_win%d" % t, tag="th_win%d" % t, align_bytes=64) for t in range(PACK)]
-        ex_win = [keep.tile([P, W + (S if t == PACK - 1 else SPARE)], F32, name="ex_win%d" % t) for t in range(PACK)]
-        nc.vector.memset(b_all[:, PACK * S :], 0.0)
-        nc.vector.memset(st2_all[:, PACK * S :], 0.0)
+        ex_win = [keep.tile([P, W + (SPARE if t == 1 else S)], F32, name="ex_win%d" % t) for t in range(PACK)]
+        st2_win = keep.tile([P, PACK, 2 * S], F32, name="st2_win")
+        st2_n4, gain_st, th_n2 = [ex_win[t][:, S:] for t in (0, 2, 3)]
+        a_n1 = [ex_win[1][:, S * (t + 1) : S * (t + 2)] for t in range(PACK - 1)] + [st2_n4[:, 2 * S + HALF : 3 * S + HALF]]
+        nc.vector.memset(ex_win[1][:, W:], 0.0)
+        for t in range(PACK):
+            nc.vector.memset(b_win[t][:, S:], 0.0)
         for t in range(PACK):
             nc.vector.memset(a_win[t][:, S:], 0.0)
-        for t in range(PACK):
-            nc.vector.memset(ex_win[t][:, S:], 0.0)
 
-        got_bytes = keep.tile([P, H + 2 * S], U8, name="got_bytes", tag="shared", align_bytes=64)
+        got_bytes = shared.tile([P, H + 2 * S], U8, name="got_bytes", offset=2 * S, align_bytes=64)
         nc.vector.tensor_copy(got_bytes[:, 0:H], d_bytes[:].indirect(k1_t[:]))
         nc.vector.tensor_copy(got_bytes[:, H : H + S], x_bytes[:].indirect(two_t[:]))
         nc.vector.tensor_copy(got_bytes[:, H + S :], x_bytes[:].indirect(offs_t[:]))
@@ -87,15 +91,17 @@ def tile_picked_kjhopphopglse_none_p_kernel(
             key_words[:].rearrange("p (t c i) -> p c t i", t=PACK, i=4),
             got_keys[:].rearrange("p (c i t) -> p c t i", t=PACK, i=4),
         )
-        two_words = keep.tile([P, S], U32, name="two_words", tag="picked", align_bytes=64)
+        two_words = keep.tile([P, S], U32, name="two_words", align_bytes=64)
         nc.vector.tensor_copy(two_words[:], x_table[:].indirect(two_t[:]))
         key_bytes = keep.tile([P, H], U8, name="key_bytes", align_bytes=64)
         nc.vector.tensor_copy(
             key_bytes[:].rearrange("p (t m) -> p t m", t=PACK),
             placed[:, 0:H].rearrange("p (m t) -> p t m", t=PACK),
         )
+        idx_words = shared.tile([P, S], U32, name="idx_words", offset=0, align_bytes=64)
+        nc.vector.tensor_copy(idx_words[:], x_table[:].indirect(offs_t[:]))
 
-        w_first = keep.tile([P, 2, PACK, P], F32, name="w_first", tag="shared", align_bytes=64)
+        w_first = shared.tile([P, 2, PACK, P], F32, name="w_first", offset=4 * S, align_bytes=64)
         for side, w in enumerate((w1, w2)):
             nc.sync.dma_start(w_first[:, side, :, :], w[:, 0:P].rearrange("(p j) m -> p j m", j=PACK))
 
@@ -120,78 +126,81 @@ def tile_picked_kjhopphopglse_none_p_kernel(
             return ap.rearrange("p t (c i) -> p c t i", i=4)
 
         def planes(tile):
-            return tile[:, 0 : PACK * S].rearrange("p (t j) -> p t j", t=PACK)
+            return tile.rearrange("p (t j) -> p t j", t=PACK)
 
         b_acc = [score(two_words, H, t, "low%d" % t) for t in range(PACK)]
 
-        b_n3 = keep.tile([P, PACK * S], F32, name="b_n3")
         for t in range(PACK):
-            nc.vector.tensor_scalar(b_all[:, plane(t)], b_acc[t][:], gm_t[:, t : t + 1], 0.0625, ALU.mult, ALU.mult)
-        idx_words = keep.tile([P, S], U32, name="idx_words", tag="picked", align_bytes=64)
-        nc.vector.tensor_copy(idx_words[:], x_table[:].indirect(offs_t[:]))
+            if t == 1:
+                nc.scalar.activation(b_win[t][:, 0:S], b_acc[t][:], ACT.Copy, scale=gm16[:, t : t + 1])
+            else:
+                nc.vector.tensor_scalar(b_win[t][:, 0:S], b_acc[t][:], gm16[:, t : t + 1], None, ALU.mult)
         a_acc = [score(idx_words, H + S, t, "high%d" % t) for t in range(PACK)]
+        for t in range(3):
+            nc.vector.tensor_scalar(a_win[t][:, 0:S], a_acc[t][:], 0.0625, None, ALU.mult)
         w_rest = keep.tile([P, 2, PACK, N - P], F32, name="w_rest", tag="shared_x")
         for side, w in enumerate((w1, w2)):
             nc.sync.dma_start(w_rest[:, side, :, :], w[:, P:].rearrange("(p j) m -> p j m", j=PACK))
 
-        def quantise_weights(mt):
+        def weave_weights(mt):
             raw = w_first[:] if mt == 0 else w_rest[:, :, :, P * (mt - 1) : P * mt]
-            words = ring.tile([P, 2 * P], U32, name="w_words", align_bytes=64)
-            scale_bytes = ring.tile([P, 2 * P], U8, name="w_bytes", align_bytes=64)
+            tag = ("first", "th_win3", "z_in", "z_in")[mt]
+            grouped = keep.tile([P, 2, P, PACK], BF16, name="grouped", tag=tag, align_bytes=64)
             if mt == 1:
-                grouped = keep.tile([P, 2, P, PACK], BF16, name="grouped1", tag="th_win3", align_bytes=64)
                 for side in range(2):
                     nc.scalar.copy(
                         grouped[:, side, :, :].rearrange("p (c i) j -> p c j i", i=4),
                         raw[:, side, :, :].rearrange("p j (c i) -> p c j i", i=4),
                     )
             else:
-                grouped = keep.tile([P, 2, P, PACK], BF16, name="grouped", tag="z_in" if mt else "first", align_bytes=64)
-                nc.vector.tensor_copy(
+                (nc.vector if mt else nc.gpsimd).tensor_copy(
                     grouped[:].rearrange("p w (c i) j -> p w c j i", i=4),
                     raw.rearrange("p w j (c i) -> p w c j i", i=4),
                 )
+            return grouped
+
+        def quantise_weights(grouped, tag):
+            words = keep.tile([P, 2 * P], U32, name="w_words", tag=tag, align_bytes=64)
+            scale_bytes = ring.tile([P, 2 * P], U8, name="w_bytes", align_bytes=64)
             nc.vector.quantize_mx(words[:].bitcast(FP8X4), scale_bytes[:], grouped[:].rearrange("p w m j -> p (w m j)"))
             return words, scale_bytes
 
-        weights = [quantise_weights(0)]
+        first_grouped = weave_weights(0)
         for t in range(PACK):
-            nc.scalar.activation(b_n3[:, plane(t)], b_all[:, S * t : S * (t + 2)].indirect(n3_t[:]), ACT.Copy)
-        st2_n4 = keep.tile([P, PACK * S], F32, name="st2_n4")
-        for u in range(2):
-            pair = slice(2 * S * u, 2 * S * (u + 1))
-            nc.vector.scalar_tensor_tensor(st2_all[:, pair], b_n3[:, pair], 0.5, b_all[:, pair], ALU.mult, ALU.add)
-            for t in ((0,), (1, 2, 3))[u]:
-                nc.vector.tensor_copy(st2_n4[:, plane(t)], st2_all[:, S * t : S * (t + 2)].indirect(n4_t[:]))
+            nc.scalar.activation(st2_win[:, t, S:], b_win[t][:].indirect(n3_t[:]), ACT.Copy)
+            nc.vector.scalar_tensor_tensor(st2_win[:, t, 0:S], st2_win[:, t, S:], 0.5, b_win[t][:, 0:S], ALU.mult, ALU.add)
+        for t in range(2):
+            nc.vector.tensor_copy(st2_n4[:, plane(t)], st2_win[:, t, :].indirect(n4_t[:]))
 
-        a_n1 = keep.tile([P, PACK * S], F32, name="a_n1")
-        gain_st = keep.tile([P, PACK * S], F32, name="gain_st")
-        th_n2 = keep.tile([P, PACK * S], F32, name="th_n2")
-        for t in range(PACK):
+        for t in range(3, PACK):
             nc.scalar.activation(a_win[t][:, 0:S], a_acc[t][:], ACT.Copy, scale=0.0625)
         for t in range(PACK):
-            nc.scalar.activation(a_n1[:, plane(t)], a_win[t][:].indirect(n1_t[:]), ACT.Copy)
-            nc.vector.tensor_tensor(th_win[t][:, S:], a_win[t][:, 0:S], a_n1[:, plane(t)], ALU.add)
+            nc.scalar.activation(a_n1[t], a_win[t][:].indirect(n1_t[:]), ACT.Copy)
+            nc.vector.scalar_tensor_tensor(th_win[t][:, S:], a_acc[t][:], 0.0625, a_n1[t], ALU.mult, ALU.add)
 
+        for t in range(2, PACK):
+            nc.vector.tensor_copy(st2_n4[:, plane(t)], st2_win[:, t, :].indirect(n4_t[:]))
         z2_in = keep.tile([P, S, PACK], BF16, name="z2_in", align_bytes=64)
         z2_words = keep.tile([P, S], U32, name="z2_words", align_bytes=64)
         z2_bytes = keep.tile([P, S], U8, name="z2_bytes", align_bytes=64)
         nc.vector.tensor_tensor(
-            z2_in[:].rearrange("p (c i) t -> p c t i", i=4), woven(planes(st2_all)), woven(planes(st2_n4)), ALU.subtract
+            z2_in[:].rearrange("p (c i) t -> p c t i", i=4), woven(st2_win[:, :, 0:S]), woven(planes(st2_n4)), ALU.subtract
         )
         for t in range(PACK):
             nc.scalar.activation(th_win[t][:, 0:S], th_win[t][:, S:], ACT.Tanh)
-            nc.vector.tensor_scalar(gain_st[:, plane(t)], th_win[t][:, S:], gn_t[:, t : t + 1], None, ALU.mult)
+            nc.gpsimd.tensor_scalar(gain_st[:, plane(t)], th_win[t][:, S:], gn_t[:, t : t + 1], 0.0, ALU.mult, ALU.add)
         nc.vector.quantize_mx(z2_words[:].bitcast(FP8X4), z2_bytes[:], z2_in[:].rearrange("p j t -> p (j t)"))
 
+        weights = [quantise_weights(first_grouped, "a_win2")]
         z_in = keep.tile([P, S, PACK], BF16, name="z_in", tag="z_in", align_bytes=64)
         z_words = keep.tile([P, S], U32, name="z_words", align_bytes=64)
         z_bytes = keep.tile([P, S], U8, name="z_bytes", align_bytes=64)
+        for t in range(PACK - 1):
+            nc.scalar.activation(th_n2[:, plane(t)], th_win[t][:].indirect(n2_t[:]), ACT.Copy)
         for u in range(2):
             cols = slice(HALF * u, HALF * (u + 1))
             entries = slice(HALF * u // 16, HALF * (u + 1) // 16)
-            for t in range(PACK):
-                nc.scalar.activation(planes(th_n2)[:, t, cols], th_win[t][:].indirect(n2_t[:, entries]), ACT.Copy)
+            nc.scalar.activation(planes(th_n2)[:, PACK - 1, cols], th_win[PACK - 1][:].indirect(n2_t[:, entries]), ACT.Copy)
             nc.vector.tensor_tensor(
                 z_in[:, cols, :].rearrange("p (c i) t -> p c t i", i=4),
                 woven(planes(gain_st)[:, :, cols]),
@@ -204,7 +213,8 @@ def tile_picked_kjhopphopglse_none_p_kernel(
 
         total = keep.tile([P, PACK * S], F32, name="total")
         h_acc = []
-        for mt in range(PACK):
+
+        def exponentials(mt):
             words, scale_bytes = weights[mt]
             h = psum.tile([P, S], F32, name="h", tag="low%d" % mt)
             h_acc.append(h)
@@ -219,18 +229,28 @@ def tile_picked_kjhopphopglse_none_p_kernel(
                     start=(side == 1),
                     stop=(side == 0),
                 )
-            if mt + 1 < PACK:
-                weights.append(quantise_weights(mt + 1))
             nc.scalar.activation(ex_win[mt][:, 0:S], h[:], ACT.Exp)
+
+        def member_sums(mt):
             sums = ring.tile([P, S], F32, name="sums")
             members = ring.tile([P, W], F32, name="members")
             nc.scalar.activation(members[:], ex_win[mt][:].indirect(n5_t[:]), ACT.Copy)
             nc.vector.tensor_reduce(sums[:], members[:].rearrange("p (j t) -> p j t", t=MEMBERS), AXIS.X, ALU.add)
             nc.vector.tensor_tensor(total[:, plane(mt)], sums[:], ex_win[mt][:, 0:S], ALU.add)
 
-        logs = ex_win[PACK - 1][:, S:]
+        for mt in range(1, PACK):
+            weights.append(quantise_weights(weave_weights(mt), "w_words%d" % mt))
+        exponentials(0)
         for mt in range(PACK):
-            nc.scalar.activation(logs[:, plane(mt)], total[:, plane(mt)], ACT.Ln)
-            result = ring.tile([P, S], F32, name="result")
-            nc.vector.tensor_tensor(result[:], logs[:, plane(mt)], h_acc[mt][:], ALU.subtract)
-            nc.sync.dma_start(out[P * mt : P * (mt + 1), :], result[:])
+            if mt + 1 < PACK:
+                exponentials(mt + 1)
+            member_sums(mt)
+
+        logs = ex_win[PACK - 1][:, S:]
+        pieces = [(mt, slice(0, S)) for mt in range(PACK - 1)]
+        pieces.extend((PACK - 1, slice(HALF * u, HALF * (u + 1))) for u in range(2))
+        result = keep.tile([P, PACK * S], F32, name="result")
+        for mt, cols in pieces:
+            nc.scalar.activation(planes(logs)[:, mt, cols], planes(total[:])[:, mt, cols], ACT.Ln)
+            nc.vector.tensor_tensor(planes(result[:])[:, mt, cols], planes(logs)[:, mt, cols], h_acc[mt][:, cols], ALU.subtract)
+            nc.sync.dma_start(out[P * mt : P * (mt + 1), cols], planes(result[:])[:, mt, cols])

@@ -60,8 +60,6 @@ def tile_picked_kjhopphopglse_none_p_kernel(
         gm_t = keep.tile([P, PACK], F32, name="gm_t")
         nc.gpsimd.dma_start(gm_t[:], gm.rearrange("(p t) o -> p (t o)", t=PACK))
         nc.gpsimd.dma_start(gn_t[:], gn.rearrange("(p t) o -> p (t o)", t=PACK))
-        gm16 = keep.tile([P, PACK], F32, name="gm16")
-        nc.scalar.activation(gm16[:], gm_t[:], ACT.Copy, scale=0.0625)
 
         placed = keep.tile([P, H + 2 * S], U8, name="placed", align_bytes=64)
         nc.vector.memset(placed[:].bitcast(I32), 0)
@@ -131,10 +129,7 @@ def tile_picked_kjhopphopglse_none_p_kernel(
         b_acc = [score(two_words, H, t, "low%d" % t) for t in range(PACK)]
 
         for t in range(PACK):
-            if t == 1:
-                nc.scalar.activation(b_win[t][:, 0:S], b_acc[t][:], ACT.Copy, scale=gm16[:, t : t + 1])
-            else:
-                nc.vector.tensor_scalar(b_win[t][:, 0:S], b_acc[t][:], gm16[:, t : t + 1], None, ALU.mult)
+            nc.vector.tensor_scalar(b_win[t][:, 0:S], b_acc[t][:], gm_t[:, t : t + 1], 0.0625, ALU.mult, ALU.mult)
         a_acc = [score(idx_words, H + S, t, "high%d" % t) for t in range(PACK)]
         for t in range(3):
             nc.vector.tensor_scalar(a_win[t][:, 0:S], a_acc[t][:], 0.0625, None, ALU.mult)
@@ -195,12 +190,11 @@ def tile_picked_kjhopphopglse_none_p_kernel(
         z_in = keep.tile([P, S, PACK], BF16, name="z_in", tag="z_in", align_bytes=64)
         z_words = keep.tile([P, S], U32, name="z_words", align_bytes=64)
         z_bytes = keep.tile([P, S], U8, name="z_bytes", align_bytes=64)
-        for t in range(PACK - 1):
-            nc.scalar.activation(th_n2[:, plane(t)], th_win[t][:].indirect(n2_t[:]), ACT.Copy)
         for u in range(2):
             cols = slice(HALF * u, HALF * (u + 1))
             entries = slice(HALF * u // 16, HALF * (u + 1) // 16)
-            nc.scalar.activation(planes(th_n2)[:, PACK - 1, cols], th_win[PACK - 1][:].indirect(n2_t[:, entries]), ACT.Copy)
+            for t in range(PACK):
+                nc.scalar.activation(planes(th_n2)[:, t, cols], th_win[t][:].indirect(n2_t[:, entries]), ACT.Copy)
             nc.vector.tensor_tensor(
                 z_in[:, cols, :].rearrange("p (c i) t -> p c t i", i=4),
                 woven(planes(gain_st)[:, :, cols]),

from contextlib import ExitStack

import concourse.mybir as mybir

K, T, S, N, G, H, W = 512, 1024, 256, 512, 2048, 512, 1024
FLOPS = 2 * K * H * S * 2 + 2 * H * N * S * 2

F32 = mybir.dt.float32
BF16 = mybir.dt.bfloat16
I32 = mybir.dt.int32
U32 = mybir.dt.uint32
U16 = mybir.dt.uint16
U8 = mybir.dt.uint8
FP8X4 = mybir.dt.float8_e4m3fn_x4
ACT = mybir.ActivationFunctionType
ALU = mybir.AluOpType
AXIS = mybir.AxisListType

P = 128
PACK = 4
HALF = S // 2
MEMBERS = W // S
SPARE = 16


def tile_picked_kjhopphopglse_none_p_kernel(
    tc, x_words, x_scales, d_words, d_scales, gn, gm, w1, w2, offs, k1, two, n1, n2, n3, n4, n5, out
):
    nc = tc.nc
    with ExitStack() as ctx:
        lists = ctx.enter_context(tc.tile_pool(name="lists", bufs=1))
        keep = ctx.enter_context(tc.tile_pool(name="keep", bufs=1))
        ring = ctx.enter_context(tc.tile_pool(name="ring", bufs=4))
        shared = ctx.enter_context(tc.tile_pool(name="shared", bufs=1))
        psum = ctx.enter_context(tc.psum_pool(name="psum", bufs=1))

        def load_list(ap, name):
            tile = lists.tile(list(ap.shape), U16, name=name)
            nc.sync.dma_start(tile[:], ap)
            return tile

        d_bytes = keep.tile([P, G], U8, name="d_bytes")
        x_bytes = keep.tile([P, T], U8, name="x_bytes")
        d_table = keep.tile([P, G], U32, name="d_table")
        x_table = keep.tile([P, T], U32, name="x_table", tag="shared_x")
        k1_t = load_list(k1, "k1_t")
        nc.sync.dma_start(d_bytes[:].bitcast(I32), d_scales[0].bitcast(I32).unsqueeze(1).to_broadcast([16, 8, G // 4]))
        two_t = load_list(two, "two_t")
        nc.sync.dma_start(x_bytes[:].bitcast(I32), x_scales[0].bitcast(I32).unsqueeze(1).to_broadcast([16, 8, T // 4]))
        offs_t = load_list(offs, "offs_t")
        n3_t = load_list(n3, "n3_t")
        n4_t = load_list(n4, "n4_t")
        nc.sync.dma_start(d_table[:].bitcast(I32), d_words[0].rearrange("p n t -> p (n t)").bitcast(I32))
        nc.sync.dma_start(x_table[:].bitcast(I32), x_words[0].rearrange("p n t -> p (n t)").bitcast(I32))
        n1_t = load_list(n1, "n1_t")
        n2_t = load_list(n2, "n2_t")
        n5_t = load_list(n5, "n5_t")

        gn_t = keep.tile([P, PACK], F32, name="gn_t")
        gm_t = keep.tile([P, PACK], F32, name="gm_t")
        nc.gpsimd.dma_start(gm_t[:], gm.rearrange("(p t) o -> p (t o)", t=PACK))
        nc.gpsimd.dma_start(gn_t[:], gn.rearrange("(p t) o -> p (t o)", t=PACK))

        placed = keep.tile([P, H + 2 * S], U8, name="placed", align_bytes=64)
        nc.vector.memset(placed[:].bitcast(I32), 0)
        b_win = [keep.tile([P, S + SPARE], F32, name="b_win%d" % t) for t in range(PACK)]
        a_win = [keep.tile([P, 2 * S], F32, name="a_win%d" % t, tag="a_win%d" % t, align_bytes=64) for t in range(PACK)]
        th_win = [keep.tile([P, 2 * S], F32, name="th_win%d" % t, tag="th_win%d" % t, align_bytes=64) for t in range(PACK)]
        ex_win = [keep.tile([P, W + (SPARE if t == 1 else S)], F32, name="ex_win%d" % t) for t in range(PACK)]
        st2_win = keep.tile([P, PACK, 2 * S], F32, name="st2_win")
        st2_n4, gain_st, th_n2 = [ex_win[t][:, S:] for t in (0, 2, 3)]
        a_n1 = [ex_win[1][:, S * (t + 1) : S * (t + 2)] for t in range(PACK - 1)] + [st2_n4[:, 2 * S + HALF : 3 * S + HALF]]
        nc.vector.memset(ex_win[1][:, W:], 0.0)
        for t in range(PACK):
            nc.vector.memset(b_win[t][:, S:], 0.0)
        for t in range(PACK):
            nc.vector.memset(a_win[t][:, S:], 0.0)

        got_bytes = shared.tile([P, H + 2 * S], U8, name="got_bytes", offset=2 * S, align_bytes=64)
        nc.vector.tensor_copy(got_bytes[:, 0:H], d_bytes[:].indirect(k1_t[:]))
        nc.vector.tensor_copy(got_bytes[:, H : H + S], x_bytes[:].indirect(two_t[:]))
        nc.vector.tensor_copy(got_bytes[:, H + S :], x_bytes[:].indirect(offs_t[:]))
        for r in range(4):
            nc.sync.dma_start(placed[r:P:32, :].bitcast(I32), got_bytes[8 * r : P : 32, :].bitcast(I32))
        got_keys = keep.tile([P, H], U32, name="got_keys")
        nc.vector.tensor_copy(got_keys[:], d_table[:].indirect(k1_t[:]))
        key_words = keep.tile([P, H], U32, name="key_words", align_bytes=64)
        nc.vector.tensor_copy(
            key_words[:].rearrange("p (t c i) -> p c t i", t=PACK, i=4),
            got_keys[:].rearrange("p (c i t) -> p c t i", t=PACK, i=4),
        )
        two_words = keep.tile([P, S], U32, name="two_words", align_bytes=64)
        nc.vector.tensor_copy(two_words[:], x_table[:].indirect(two_t[:]))
        key_bytes = keep.tile([P, H], U8, name="key_bytes", align_bytes=64)
        nc.vector.tensor_copy(
            key_bytes[:].rearrange("p (t m) -> p t m", t=PACK),
            placed[:, 0:H].rearrange("p (m t) -> p t m", t=PACK),
        )
        idx_words = shared.tile([P, S], U32, name="idx_words", offset=0, align_bytes=64)
        nc.vector.tensor_copy(idx_words[:], x_table[:].indirect(offs_t[:]))

        w_first = shared.tile([P, 2, PACK, P], F32, name="w_first", offset=4 * S, align_bytes=64)
        for side, w in enumerate((w1, w2)):
            nc.sync.dma_start(w_first[:, side, :, :], w[:, 0:P].rearrange("(p j) m -> p j m", j=PACK))

        def score(words, first_byte, t, tag):
            acc = psum.tile([P, S], F32, name="acc", tag=tag)
            rows = slice(P * t, P * (t + 1))
            nc.tensor.matmul_mx(
                out=acc[:],
                lhsT=key_words[:, rows].bitcast(FP8X4),
                lhsT_scale=key_bytes[:, rows],
                rhs=words[:].bitcast(FP8X4),
                rhs_scale=placed[:, first_byte : first_byte + S],
                start=True,
                stop=True,
            )
            return acc

        def plane(t):
            return slice(S * t, S * (t + 1))

        def woven(ap):
            return ap.rearrange("p t (c i) -> p c t i", i=4)

        def planes(tile):
            return tile.rearrange("p (t j) -> p t j", t=PACK)

        b_acc = [score(two_words, H, t, "low%d" % t) for t in range(PACK)]

        for t in range(PACK):
            nc.vector.tensor_scalar(b_win[t][:, 0:S], b_acc[t][:], gm_t[:, t : t + 1], 0.0625, ALU.mult, ALU.mult)
        a_acc = [score(idx_words, H + S, t, "high%d" % t) for t in range(PACK)]
        for t in range(3):
            nc.vector.tensor_scalar(a_win[t][:, 0:S], a_acc[t][:], 0.0625, None, ALU.mult)
        w_rest = keep.tile([P, 2, PACK, N - P], F32, name="w_rest", tag="shared_x")
        for side, w in enumerate((w1, w2)):
            nc.sync.dma_start(w_rest[:, side, :, :], w[:, P:].rearrange("(p j) m -> p j m", j=PACK))

        def weave_weights(mt):
            raw = w_first[:] if mt == 0 else w_rest[:, :, :, P * (mt - 1) : P * mt]
            tag = ("first", "th_win3", "z_in", "z_in")[mt]
            grouped = keep.tile([P, 2, P, PACK], BF16, name="grouped", tag=tag, align_bytes=64)
            if mt == 1:
                for side in range(2):
                    nc.scalar.copy(
                        grouped[:, side, :, :].rearrange("p (c i) j -> p c j i", i=4),
                        raw[:, side, :, :].rearrange("p j (c i) -> p c j i", i=4),
                    )
            else:
                (nc.vector if mt else nc.gpsimd).tensor_copy(
                    grouped[:].rearrange("p w (c i) j -> p w c j i", i=4),
                    raw.rearrange("p w j (c i) -> p w c j i", i=4),
                )
            return grouped

        def quantise_weights(grouped, tag):
            words = keep.tile([P, 2 * P], U32, name="w_words", tag=tag, align_bytes=64)
            scale_bytes = ring.tile([P, 2 * P], U8, name="w_bytes", align_bytes=64)
            nc.vector.quantize_mx(words[:].bitcast(FP8X4), scale_bytes[:], grouped[:].rearrange("p w m j -> p (w m j)"))
            return words, scale_bytes

        first_grouped = weave_weights(0)
        for t in range(PACK):
            nc.scalar.activation(st2_win[:, t, S:], b_win[t][:].indirect(n3_t[:]), ACT.Copy)
            nc.vector.scalar_tensor_tensor(st2_win[:, t, 0:S], st2_win[:, t, S:], 0.5, b_win[t][:, 0:S], ALU.mult, ALU.add)
        for t in range(2):
            nc.vector.tensor_copy(st2_n4[:, plane(t)], st2_win[:, t, :].indirect(n4_t[:]))

        for t in range(3, PACK):
            nc.scalar.activation(a_win[t][:, 0:S], a_acc[t][:], ACT.Copy, scale=0.0625)
        for t in range(PACK):
            nc.scalar.activation(a_n1[t], a_win[t][:].indirect(n1_t[:]), ACT.Copy)
            nc.vector.scalar_tensor_tensor(th_win[t][:, S:], a_acc[t][:], 0.0625, a_n1[t], ALU.mult, ALU.add)

        for t in range(2, PACK):
            nc.vector.tensor_copy(st2_n4[:, plane(t)], st2_win[:, t, :].indirect(n4_t[:]))
        z2_in = keep.tile([P, S, PACK], BF16, name="z2_in", align_bytes=64)
        z2_words = keep.tile([P, S], U32, name="z2_words", align_bytes=64)
        z2_bytes = keep.tile([P, S], U8, name="z2_bytes", align_bytes=64)
        nc.vector.tensor_tensor(
            z2_in[:].rearrange("p (c i) t -> p c t i", i=4), woven(st2_win[:, :, 0:S]), woven(planes(st2_n4)), ALU.subtract
        )
        for t in range(PACK):
            nc.scalar.activation(th_win[t][:, 0:S], th_win[t][:, S:], ACT.Tanh)
            nc.gpsimd.tensor_scalar(gain_st[:, plane(t)], th_win[t][:, S:], gn_t[:, t : t + 1], 0.0, ALU.mult, ALU.add)
        nc.vector.quantize_mx(z2_words[:].bitcast(FP8X4), z2_bytes[:], z2_in[:].rearrange("p j t -> p (j t)"))

        weights = [quantise_weights(first_grouped, "a_win2")]
        z_in = keep.tile([P, S, PACK], BF16, name="z_in", tag="z_in", align_bytes=64)
        z_words = keep.tile([P, S], U32, name="z_words", align_bytes=64)
        z_bytes = keep.tile([P, S], U8, name="z_bytes", align_bytes=64)
        for u in range(2):
            cols = slice(HALF * u, HALF * (u + 1))
            entries = slice(HALF * u // 16, HALF * (u + 1) // 16)
            for t in range(PACK):
                nc.scalar.activation(planes(th_n2)[:, t, cols], th_win[t][:].indirect(n2_t[:, entries]), ACT.Copy)
            nc.vector.tensor_tensor(
                z_in[:, cols, :].rearrange("p (c i) t -> p c t i", i=4),
                woven(planes(gain_st)[:, :, cols]),
                woven(planes(th_n2)[:, :, cols]),
                ALU.mult,
            )
            nc.vector.quantize_mx(
                z_words[:, cols].bitcast(FP8X4), z_bytes[:, cols], z_in[:, cols, :].rearrange("p j t -> p (j t)")
            )

        total = keep.tile([P, PACK * S], F32, name="total")
        h_acc = []

        def exponentials(mt):
            words, scale_bytes = weights[mt]
            h = psum.tile([P, S], F32, name="h", tag="low%d" % mt)
            h_acc.append(h)
            for side, (rhs, rhs_scale) in ((1, (z2_words, z2_bytes)), (0, (z_words, z_bytes))):
                cols = slice(P * side, P * (side + 1))
                nc.tensor.matmul_mx(
                    out=h[:],
                    lhsT=words[:, cols].bitcast(FP8X4),
                    lhsT_scale=scale_bytes[:, cols],
                    rhs=rhs[:].bitcast(FP8X4),
                    rhs_scale=rhs_scale[:],
                    start=(side == 1),
                    stop=(side == 0),
                )
            nc.scalar.activation(ex_win[mt][:, 0:S], h[:], ACT.Exp)

        def member_sums(mt):
            sums = ring.tile([P, S], F32, name="sums")
            members = ring.tile([P, W], F32, name="members")
            nc.scalar.activation(members[:], ex_win[mt][:].indirect(n5_t[:]), ACT.Copy)
            nc.vector.tensor_reduce(sums[:], members[:].rearrange("p (j t) -> p j t", t=MEMBERS), AXIS.X, ALU.add)
            nc.vector.tensor_tensor(total[:, plane(mt)], sums[:], ex_win[mt][:, 0:S], ALU.add)

        for mt in range(1, PACK):
            weights.append(quantise_weights(weave_weights(mt), "w_words%d" % mt))
        exponentials(0)
        for mt in range(PACK):
            if mt + 1 < PACK:
                exponentials(mt + 1)
            member_sums(mt)

        logs = ex_win[PACK - 1][:, S:]
        pieces = [(mt, slice(0, S)) for mt in range(PACK - 1)]
        pieces.extend((PACK - 1, slice(HALF * u, HALF * (u + 1))) for u in range(2))
        result = keep.tile([P, PACK * S], F32, name="result")
        for mt, cols in pieces:
            nc.scalar.activation(planes(logs)[:, mt, cols], planes(total[:])[:, mt, cols], ACT.Ln)
            nc.vector.tensor_tensor(planes(result[:])[:, mt, cols], planes(logs)[:, mt, cols], h_acc[mt][:, cols], ALU.subtract)
            nc.sync.dma_start(out[P * mt : P * (mt + 1), cols], planes(result[:])[:, mt, cols])
